import numpy as np
CORES = [10,18,34,42,58,66,82,90,98,106]
N = 10
T, M = 4096, 512
def entries(a): return a.T.reshape(-1)
def pack(v, P): return np.ascontiguousarray(np.asarray(v, np.int32).reshape(-1, P).T)
def lists(rng, how):
    I = rng.integers(0, T, (N, M))
    if how == "alike": I[:] = rng.integers(0, T, (N, 1))
    if how == "distinct": I = np.stack([rng.permutation(T)[:M] for r in range(N)])
    if how == "sorted": I = np.sort(I, axis=1)
    if how == "edge": I = np.where(rng.random((N, M)) < 0.5, 0, T - 1)
    return {"idx": np.stack([pack(I[r], 16) for r in range(N)])}
def setup_inputs(rng):
    return dict({"x": rng.standard_normal((N, 128, T), dtype=np.float32)}, **lists(rng, "uniform"))
def setup_inputs_alike(rng):
    d = setup_inputs(rng); d.update(lists(rng, "alike"))
    for k in ("x",): d[k] = (d[k].astype(np.float32) * 1024.0).astype(d[k].dtype)
    return d
def setup_inputs_distinct(rng):
    d = setup_inputs(rng); d.update(lists(rng, "distinct"))
    for k in ("x",): d[k] = (d[k].astype(np.float32) * (1 / 1024.0)).astype(d[k].dtype)
    return d
def setup_inputs_edge(rng):
    d = setup_inputs(rng); d.update(lists(rng, "edge"))
    return d
def setup_inputs_sorted(rng):
    d = setup_inputs(rng); d.update(lists(rng, "sorted"))
    return d
def check_inputs(x):
    bad = []
    if x["idx"].min() < 0 or x["idx"].max() >= T: bad.append("idx out of range")
    return bad
def reference(x, idx):
    s = sum(x[r].astype(np.float64)[:, entries(idx[r])] for r in range(N)).astype(np.float32)
    return {"y": np.broadcast_to(s, (N, 128, M))}

@@ -1,0 +1,206 @@
+from concourse.bass import DstId, RemoteDMATransfer
+from concourse.mybir import AluOpType, ActivationFunctionType
+
+N = 10
+P = 128
+TC = 4096
+M = 512
+GRP = 16
+LOW = P // N
+HIGH = LOW + 1
+NA = P - LOW * N
+NB = N - NA
+WA = HIGH * M // P
+WB = LOW * M // P
+H = M // 2
+
+SCRATCH = {
+    "xs": ("sbuf", [P, TC], "float32"),
+    "idxi": ("sbuf", [P, M // GRP], "int32"),
+    "idxf": ("sbuf", [P, M // GRP], "float32"),
+    "off": ("sbuf", [P, M // GRP], "uint16"),
+    "ones": ("sbuf", [P, P], "float32"),
+    "rep": ("sbuf", [P, P], "float32"),
+    "repn": ("sbuf", [P, (N - 1) * HIGH], "float32"),
+    "selown": ("sbuf", [P, HIGH], "float32"),
+    "selsum": ("sbuf", [P, HIGH], "float32"),
+    "gat": ("sbuf", [P, M], "float32"),
+    "slots": ("sbuf", [P, M], "float32"),
+    "mine": ("sbuf", [P, M], "float32"),
+    "stage_a": ("dram", [NA, P, WA], "float32"),
+    "stage_b": ("dram", [NB, P, WB], "float32"),
+    "land_a": ("dram", [N - 1, P, WA], "float32"),
+    "land_b": ("dram", [N - 1, P, WB], "float32"),
+    "res_a": ("dram", [NA, P, WA], "float32"),
+    "res_b": ("dram", [NB, P, WB], "float32"),
+    "ps_i": ("psum", [P, M], "float32"),
+    "ps_s": ("psum", [P, M], "float32"),
+    "ps_lo": ("psum", [P, M], "float32"),
+    "ps_hi": ("psum", [P, M], "float32"),
+}
+SEMAPHORES = ["s_idx", "s_x", "s_one", "s_rep", "s_repn", "s_selown", "s_idxf", "s_psi", "s_off", "s_pss", "s_sel",
+              "s_gv", "s_gs", "s_da", "s_db", "rs", "ag", "sent", "s_slots", "s_mlo", "s_mhi", "s_mine", "s_st"]
+
+
+def _bits(mask):
+    return [b for b in range(16) if (mask >> b) & 1]
+
+
+def _to_mask(engines):
+    m = 0
+    for b in engines:
+        m |= 1 << b
+    return m
+
+
+def _engines(topo, cores, r):
+    m = None
+    for d in range(N):
+        if d != r:
+            if not topo.may_write(cores[r], cores[d]):
+                raise ValueError("rank %d may not write to rank %d" % (r, d))
+            mm = topo.mask(cores[r], cores[d])
+            m = mm if m is None else (m & mm)
+    return _bits(m)
+
+
+def _rs_plan(topo, cores, r):
+    e = _engines(topo, cores, r)
+    a = [d for d in range(NA) if d != r]
+    b = [d for d in range(NA, N) if d != r]
+    wide = [(d, [e[i]]) for i, d in enumerate(a)]
+    if len(b) == 1:
+        narrow = [(b[0], list(e))]
+    else:
+        o = b if r % 2 == 0 else b[::-1]
+        narrow = [(o[0], e[len(a):len(a) + 1]),
+                  (o[1], e[0::2])]
+    return wide, narrow
+
+
+def rank_program(g, core, T, topo):
+    k = T.rank_of(core)
+    if k is None:
+        return
+    sem = T.sem
+    cores = T.cores
+    v, s, pe, sy = g.vector, g.scalar, g.tensor, g.sync
+
+    wide_owner = k < NA
+    n = HIGH if wide_owner else LOW
+    r0 = k * HIGH if wide_owner else NA * HIGH + (k - NA) * LOW
+    kn = (N - 1) * n
+    my_stage = T.stage_a[k] if wide_owner else T.stage_b[k - NA]
+    my_land = T.land_a if wide_owner else T.land_b
+    my_res = T.res_a[k] if wide_owner else T.res_b[k - NA]
+
+    def dst_id(d):
+        rid, pid, _ = topo.addr(cores[d])
+        return DstId(rid=rid, pnc=pid)
+
+    rs_total = 0
+    for r in range(N):
+        if r != k:
+            wide, narrow = _rs_plan(topo, cores, r)
+            rs_total += sum(len(e) for d, e in wide + narrow if d == k)
+    wide, narrow = _rs_plan(topo, cores, k)
+    eng = _engines(topo, cores, k)
+    ag_total = (N - 1) * len(eng)
+    sent_total = sum(len(e) for d, e in wide + narrow) + len(eng)
+
+    sy.dma_start(T.idxi[0:GRP, :], T.idx[:, :]).then_inc(sem.s_idx, 16)
+    sy.dma_start(T.xs[:, :], T.x[:, :]).then_inc(sem.s_x, 16)
+    sy.wait_ge(sem.s_gv, 1)
+    sy.wait_ge(sem.s_gs, 1)
+    sy.dma_start(T.stage_a[:, :, :], T.gat[0:NA * HIGH, :]).then_inc(sem.s_da, 16)
+    sy.wait_ge(sem.rs, rs_total)
+    sy.dma_start(T.slots[0:kn, :], my_land[:, :, :]).then_inc(sem.s_slots, 16)
+    stores = 0
+    sy.wait_ge(sem.ag, ag_total)
+    runs = [(0, k), (k + 1, NA)] if wide_owner else [(0, NA)]
+    runs = sorted([x for x in runs if x[1] > x[0]], key=lambda x: x[0] - x[1])
+    for lo, hi in runs:
+        sy.dma_start(T.y[lo * HIGH:hi * HIGH, :], T.res_a[lo:hi]).then_inc(sem.s_st, 16)
+        stores += 1
+
+    v.memset(T.ones[:, :], 1.0).then_inc(sem.s_one, 1)
+    v.wait_ge(sem.s_idx, 16)
+    v.tensor_copy(T.idxf[0:GRP, :], T.idxi[0:GRP, :]).then_inc(sem.s_idxf, 1)
+    v.wait_ge(sem.s_psi, 1)
+    v.tensor_copy(T.off[:, :], T.ps_i[:, 0:M // GRP]).then_inc(sem.s_off, 1)
+    v.wait_ge(sem.s_pss, 1)
+    v.tensor_copy(T.selsum[0:kn, 0:n], T.ps_s[0:kn, 0:n]).then_inc(sem.s_sel, 1)
+    v.wait_ge(sem.s_off, 1)
+    v.wait_ge(sem.s_x, 16)
+    v.tensor_copy(T.gat[:, 0:H], T.xs[:, 0:TC].indirect(T.off[:, 0:H // GRP])).then_inc(sem.s_gv, 1)
+    v.wait_ge(sem.s_mlo, 1)
+    v.tensor_copy(T.mine[0:n, 0:H], T.ps_lo[0:n, 0:H]).then_inc(sem.s_mine, 1)
+    v.wait_ge(sem.s_mhi, 1)
+    v.tensor_copy(T.mine[0:n, H:M], T.ps_hi[0:n, 0:H]).then_inc(sem.s_mine, 1)
+
+    s.wait_ge(sem.s_off, 1)
+    s.wait_ge(sem.s_x, 16)
+    s.activation(T.gat[:, H:M], T.xs[:, 0:TC].indirect(T.off[:, H // GRP:M // GRP]),
+                 ActivationFunctionType.Copy).then_inc(sem.s_gs, 1)
+    s.wait_ge(sem.s_gs, 1)
+    s.wait_ge(sem.s_gv, 1)
+    s.dma_start(T.stage_b[:, :, :], T.gat[NA * HIGH:P, :]).then_inc(sem.s_db, 16)
+    s.wait_ge(sem.ag, ag_total)
+    runs = [(0, NB)] if wide_owner else [(0, k - NA), (k - NA + 1, NB)]
+    for lo, hi in runs:
+        if hi > lo:
+            s.dma_start(T.y[NA * HIGH + lo * LOW:NA * HIGH + hi * LOW, :], T.res_b[lo:hi]).then_inc(sem.s_st, 16)
+            stores += 1
+    s.wait_ge(sem.s_mine, 2)
+    s.dma_start(T.y[r0:r0 + n, :], T.mine[0:n, :]).then_inc(sem.s_st, 16)
+    stores += 1
+
+    pe.wait_ge(sem.s_rep, 1)
+    pe.wait_ge(sem.s_idxf, 1)
+    pe.matmul(T.ps_i[:, 0:M // GRP], T.rep[0:GRP, :], T.idxf[0:GRP, :], start=True, stop=True).then_inc(sem.s_psi, 1)
+    pe.wait_ge(sem.s_repn, 1)
+    pe.matmul(T.ps_s[0:kn, 0:n], T.repn[0:n, 0:kn], T.repn[0:n, 0:n], start=True, stop=True).then_inc(sem.s_pss, 1)
+    pe.wait_ge(sem.s_selown, 1)
+    pe.wait_ge(sem.s_gv, 1)
+    pe.wait_ge(sem.s_gs, 1)
+    pe.matmul(T.ps_lo[0:n, 0:H], T.selown[:, 0:n], T.gat[:, 0:H], start=True, stop=False)
+    pe.matmul(T.ps_hi[0:n, 0:H], T.selown[:, 0:n], T.gat[:, H:M], start=True, stop=False)
+    pe.wait_ge(sem.s_sel, 1)
+    pe.wait_ge(sem.s_slots, 16)
+    pe.matmul(T.ps_lo[0:n, 0:H], T.selsum[0:kn, 0:n], T.slots[0:kn, 0:H], start=False, stop=True).then_inc(sem.s_mlo, 1)
+    pe.matmul(T.ps_hi[0:n, 0:H], T.selsum[0:kn, 0:n], T.slots[0:kn, H:M], start=False, stop=True).then_inc(sem.s_mhi, 1)
+
+    g.wait_ge(sem.s_one, 1)
+    g.affine_select(out=T.rep[0:GRP, :], in_=T.ones[0:GRP, :], pattern=[[0, P // GRP], [-1, GRP]],
+                    compare_op=AluOpType.is_equal, fill=0.0, base=0, channel_multiplier=1).then_inc(sem.s_rep, 1)
+    g.affine_select(out=T.repn[0:n, 0:kn], in_=T.ones[0:n, 0:kn], pattern=[[0, N - 1], [-1, n]],
+                    compare_op=AluOpType.is_equal, fill=0.0, base=0, channel_multiplier=1).then_inc(sem.s_repn, 1)
+    g.affine_select(out=T.selown[:, 0:n], in_=T.ones[:, 0:n], pattern=[[-1, n]],
+                    compare_op=AluOpType.is_equal, fill=0.0, base=-r0, channel_multiplier=1).then_inc(sem.s_selown, 1)
+
+    def scatter(plan):
+        trs = []
+        for d, e in plan:
+            slot = k if k < d else k - 1
+            if d < NA:
+                src, dst = T.stage_a[d], T.land_a[slot]
+            else:
+                src, dst = T.stage_b[d - NA], T.land_b[slot]
+            trs.append(RemoteDMATransfer(dst_ids=[dst_id(d)], dma_engine_mask=_to_mask(e), remote_sem=sem.rs,
+                                         src=src, dst=dst))
+        g.remote_dma_fused(trs, local_sem=sem.sent)
+
+    g.wait_ge(sem.s_db, 16)
+    scatter(narrow)
+    g.wait_ge(sem.s_da, 16)
+    scatter(wide)
+
+    g.wait_ge(sem.rs, rs_total)
+    others = [d for d in range(N) if d != k]
+    g.remote_dma_fused([RemoteDMATransfer(dst_ids=[dst_id(d) for d in others], dma_engine_mask=_to_mask(eng),
+                                          remote_sem=sem.ag,
+                                          srcs=[my_land[i] for i in range(N - 1)] + [my_stage],
+                                          dsts=[my_res for d in others], alu_op=1)],
+                       local_sem=sem.sent)
+    g.wait_ge(sem.sent, sent_total)
+    g.wait_ge(sem.s_st, 16 * stores)

@@ -2,17 +2,21 @@ from concourse.bass import DstId, RemoteDMATransfer
 from concourse.mybir import AluOpType, ActivationFunctionType
 
 N = 10
+NSIM = 112
 P = 128
 TC = 4096
 M = 512
 GRP = 16
+H = M // 2
+Q = H // 2
+NH = 8
+WH = (P // NH) * H // P
 LOW = P // N
 HIGH = LOW + 1
 NA = P - LOW * N
 NB = N - NA
-WA = HIGH * M // P
-WB = LOW * M // P
-H = M // 2
+WA = HIGH * H // P
+WB = LOW * H // P
 
 SCRATCH = {
     "xs": ("sbuf", [P, TC], "float32"),
@@ -25,8 +29,11 @@ SCRATCH = {
     "selown": ("sbuf", [P, HIGH], "float32"),
     "selsum": ("sbuf", [P, HIGH], "float32"),
     "gat": ("sbuf", [P, M], "float32"),
-    "slots": ("sbuf", [P, M], "float32"),
-    "mine": ("sbuf", [P, M], "float32"),
+    "slots": ("sbuf", [P, H], "float32"),
+    "mine": ("sbuf", [P, H], "float32"),
+    "stage_h": ("dram", [NH, P, WH], "float32"),
+    "land_h": ("dram", [N, P, WH], "float32"),
+    "res_h": ("dram", [NH, P, WH], "float32"),
     "stage_a": ("dram", [NA, P, WA], "float32"),
     "stage_b": ("dram", [NB, P, WB], "float32"),
     "land_a": ("dram", [N - 1, P, WA], "float32"),
@@ -35,11 +42,11 @@ SCRATCH = {
     "res_b": ("dram", [NB, P, WB], "float32"),
     "ps_i": ("psum", [P, M], "float32"),
     "ps_s": ("psum", [P, M], "float32"),
-    "ps_lo": ("psum", [P, M], "float32"),
-    "ps_hi": ("psum", [P, M], "float32"),
+    "ps_o": ("psum", [P, M], "float32"),
 }
 SEMAPHORES = ["s_idx", "s_x", "s_one", "s_rep", "s_repn", "s_selown", "s_idxf", "s_psi", "s_off", "s_pss", "s_sel",
-              "s_gv", "s_gs", "s_da", "s_db", "rs", "ag", "sent", "s_slots", "s_mlo", "s_mhi", "s_mine", "s_st"]
+              "s_gv0", "s_gs0", "s_gv1", "s_gs1", "s_dh", "s_da", "s_db", "rsh", "agh", "rs", "ag", "sent",
+              "s_slots", "s_m", "s_mine", "s_st"]
 
 
 def _bits(mask):
@@ -53,15 +60,28 @@ def _to_mask(engines):
     return m
 
 
-def _engines(topo, cores, r):
+def _helpers(topo, cores):
+    out = []
+    for d in range(NH):
+        c = [h for h in range(NSIM)
+             if h not in cores and topo.chip(h) == topo.chip(cores[d]) and topo.die(h) != topo.die(cores[d])
+             and all(topo.may_write(h, r) for r in cores)]
+        out.append(c[0])
+    return out
+
+
+def _common(topo, src, dsts):
     m = None
-    for d in range(N):
-        if d != r:
-            if not topo.may_write(cores[r], cores[d]):
-                raise ValueError("rank %d may not write to rank %d" % (r, d))
-            mm = topo.mask(cores[r], cores[d])
-            m = mm if m is None else (m & mm)
+    for d in dsts:
+        if not topo.may_write(src, d):
+            raise ValueError("core %d may not write to core %d" % (src, d))
+        mm = topo.mask(src, d)
+        m = mm if m is None else (m & mm)
     return _bits(m)
+
+
+def _engines(topo, cores, r):
+    return _common(topo, cores[r], [c for c in cores if c != cores[r]] + _helpers(topo, cores))
 
 
 def _rs_plan(topo, cores, r):
@@ -78,12 +98,33 @@ def _rs_plan(topo, cores, r):
     return wide, narrow
 
 
-def rank_program(g, core, T, topo):
-    k = T.rank_of(core)
-    if k is None:
-        return
+def _dst(topo, c):
+    rid, pid, _ = topo.addr(c)
+    return DstId(rid=rid, pnc=pid)
+
+
+def helper_program(g, core, T, topo, d):
     sem = T.sem
     cores = T.cores
+    e = _common(topo, core, cores)
+    g.wait_ge(sem.rsh, N)
+    g.remote_dma_fused([RemoteDMATransfer(dst_ids=[_dst(topo, c) for c in cores], dma_engine_mask=_to_mask(e),
+                                          remote_sem=sem.agh,
+                                          srcs=[T.land_h[i] for i in range(N)],
+                                          dsts=[T.res_h[d] for c in cores], alu_op=1)],
+                       local_sem=sem.sent)
+    g.wait_ge(sem.sent, len(e))
+
+
+def rank_program(g, core, T, topo):
+    cores = T.cores
+    helpers = _helpers(topo, cores)
+    k = T.rank_of(core)
+    if k is None:
+        if core in helpers:
+            helper_program(g, core, T, topo, helpers.index(core))
+        return
+    sem = T.sem
     v, s, pe, sy = g.vector, g.scalar, g.tensor, g.sync
 
     wide_owner = k < NA
@@ -94,34 +135,35 @@ def rank_program(g, core, T, topo):
     my_land = T.land_a if wide_owner else T.land_b
     my_res = T.res_a[k] if wide_owner else T.res_b[k - NA]
 
-    def dst_id(d):
-        rid, pid, _ = topo.addr(cores[d])
-        return DstId(rid=rid, pnc=pid)
-
     rs_total = 0
     for r in range(N):
         if r != k:
-            wide, narrow = _rs_plan(topo, cores, r)
-            rs_total += sum(len(e) for d, e in wide + narrow if d == k)
+            w_, n_ = _rs_plan(topo, cores, r)
+            rs_total += sum(len(e) for d, e in w_ + n_ if d == k)
     wide, narrow = _rs_plan(topo, cores, k)
     eng = _engines(topo, cores, k)
+    if len(eng) < NH:
+        raise ValueError("fewer engines than pieces of half 0")
     ag_total = (N - 1) * len(eng)
-    sent_total = sum(len(e) for d, e in wide + narrow) + len(eng)
+    agh_total = sum(len(_common(topo, h, cores)) for h in helpers)
+    sent_total = NH + sum(len(e) for d, e in wide + narrow) + len(eng)
+    stores = [0]
 
-    sy.dma_start(T.idxi[0:GRP, :], T.idx[:, :]).then_inc(sem.s_idx, 16)
-    sy.dma_start(T.xs[:, :], T.x[:, :]).then_inc(sem.s_x, 16)
-    sy.wait_ge(sem.s_gv, 1)
-    sy.wait_ge(sem.s_gs, 1)
-    sy.dma_start(T.stage_a[:, :, :], T.gat[0:NA * HIGH, :]).then_inc(sem.s_da, 16)
+    sy.dma_start(T.xs[0:P // 2, :], T.x[0:P // 2, :]).then_inc(sem.s_x, 16)
+    sy.wait_ge(sem.s_gv0, 1)
+    sy.wait_ge(sem.s_gs0, 1)
+    sy.dma_start(T.stage_h[:, :, :], T.gat[:, 0:H]).then_inc(sem.s_dh, 16)
+    sy.wait_ge(sem.s_gv1, 1)
+    sy.wait_ge(sem.s_gs1, 1)
+    sy.dma_start(T.stage_a[:, :, :], T.gat[0:NA * HIGH, H:M]).then_inc(sem.s_da, 16)
     sy.wait_ge(sem.rs, rs_total)
     sy.dma_start(T.slots[0:kn, :], my_land[:, :, :]).then_inc(sem.s_slots, 16)
-    stores = 0
-    sy.wait_ge(sem.ag, ag_total)
-    runs = [(0, k), (k + 1, NA)] if wide_owner else [(0, NA)]
-    runs = sorted([x for x in runs if x[1] > x[0]], key=lambda x: x[0] - x[1])
-    for lo, hi in runs:
-        sy.dma_start(T.y[lo * HIGH:hi * HIGH, :], T.res_a[lo:hi]).then_inc(sem.s_st, 16)
-        stores += 1
+    sy.wait_ge(sem.agh, agh_total)
+    sy.dma_start(T.y[:, 0:H], T.res_h[:, :, :]).then_inc(sem.s_st, 16)
+    stores[0] += 1
+    sy.wait_ge(sem.s_mine, 1)
+    sy.dma_start(T.y[r0:r0 + n, H:M], T.mine[0:n, :]).then_inc(sem.s_st, 16)
+    stores[0] += 1
 
     v.memset(T.ones[:, :], 1.0).then_inc(sem.s_one, 1)
     v.wait_ge(sem.s_idx, 16)
@@ -131,29 +173,36 @@ def rank_program(g, core, T, topo):
     v.wait_ge(sem.s_pss, 1)
     v.tensor_copy(T.selsum[0:kn, 0:n], T.ps_s[0:kn, 0:n]).then_inc(sem.s_sel, 1)
     v.wait_ge(sem.s_off, 1)
-    v.wait_ge(sem.s_x, 16)
-    v.tensor_copy(T.gat[:, 0:H], T.xs[:, 0:TC].indirect(T.off[:, 0:H // GRP])).then_inc(sem.s_gv, 1)
-    v.wait_ge(sem.s_mlo, 1)
-    v.tensor_copy(T.mine[0:n, 0:H], T.ps_lo[0:n, 0:H]).then_inc(sem.s_mine, 1)
-    v.wait_ge(sem.s_mhi, 1)
-    v.tensor_copy(T.mine[0:n, H:M], T.ps_hi[0:n, 0:H]).then_inc(sem.s_mine, 1)
+    v.wait_ge(sem.s_x, 32)
+    for c, done in ((0, sem.s_gv0), (1, sem.s_gv1)):
+        j = c * H
+        v.tensor_copy(T.gat[:, j:j + Q],
+                      T.xs[:, 0:TC].indirect(T.off[:, j // GRP:(j + Q) // GRP])).then_inc(done, 1)
+    v.wait_ge(sem.s_m, 1)
+    v.tensor_copy(T.mine[0:n, :], T.ps_o[0:n, 0:H]).then_inc(sem.s_mine, 1)
 
+    s.dma_start(T.idxi[0:GRP, :], T.idx[:, :]).then_inc(sem.s_idx, 16)
+    s.dma_start(T.xs[P // 2:P, :], T.x[P // 2:P, :]).then_inc(sem.s_x, 16)
     s.wait_ge(sem.s_off, 1)
-    s.wait_ge(sem.s_x, 16)
-    s.activation(T.gat[:, H:M], T.xs[:, 0:TC].indirect(T.off[:, H // GRP:M // GRP]),
-                 ActivationFunctionType.Copy).then_inc(sem.s_gs, 1)
-    s.wait_ge(sem.s_gs, 1)
-    s.wait_ge(sem.s_gv, 1)
-    s.dma_start(T.stage_b[:, :, :], T.gat[NA * HIGH:P, :]).then_inc(sem.s_db, 16)
+    s.wait_ge(sem.s_x, 32)
+    for c, done in ((0, sem.s_gs0), (1, sem.s_gs1)):
+        j = c * H + Q
+        s.activation(T.gat[:, j:j + Q], T.xs[:, 0:TC].indirect(T.off[:, j // GRP:(j + Q) // GRP]),
+                     ActivationFunctionType.Copy).then_inc(done, 1)
+    s.wait_ge(sem.s_gs1, 1)
+    s.wait_ge(sem.s_gv1, 1)
+    s.dma_start(T.stage_b[:, :, :], T.gat[NA * HIGH:P, H:M]).then_inc(sem.s_db, 16)
     s.wait_ge(sem.ag, ag_total)
-    runs = [(0, NB)] if wide_owner else [(0, k - NA), (k - NA + 1, NB)]
-    for lo, hi in runs:
+    runs_a = [(0, k), (k + 1, NA)] if wide_owner else [(0, NA)]
+    runs_a = sorted([x for x in runs_a if x[1] > x[0]], key=lambda x: x[0] - x[1])
+    for lo, hi in runs_a:
+        s.dma_start(T.y[lo * HIGH:hi * HIGH, H:M], T.res_a[lo:hi]).then_inc(sem.s_st, 16)
+        stores[0] += 1
+    runs_b = [(0, NB)] if wide_owner else [(0, k - NA), (k - NA + 1, NB)]
+    for lo, hi in runs_b:
         if hi > lo:
-            s.dma_start(T.y[NA * HIGH + lo * LOW:NA * HIGH + hi * LOW, :], T.res_b[lo:hi]).then_inc(sem.s_st, 16)
-            stores += 1
-    s.wait_ge(sem.s_mine, 2)
-    s.dma_start(T.y[r0:r0 + n, :], T.mine[0:n, :]).then_inc(sem.s_st, 16)
-    stores += 1
+            s.dma_start(T.y[NA * HIGH + lo * LOW:NA * HIGH + hi * LOW, H:M], T.res_b[lo:hi]).then_inc(sem.s_st, 16)
+            stores[0] += 1
 
     pe.wait_ge(sem.s_rep, 1)
     pe.wait_ge(sem.s_idxf, 1)
@@ -161,14 +210,12 @@ def rank_program(g, core, T, topo):
     pe.wait_ge(sem.s_repn, 1)
     pe.matmul(T.ps_s[0:kn, 0:n], T.repn[0:n, 0:kn], T.repn[0:n, 0:n], start=True, stop=True).then_inc(sem.s_pss, 1)
     pe.wait_ge(sem.s_selown, 1)
-    pe.wait_ge(sem.s_gv, 1)
-    pe.wait_ge(sem.s_gs, 1)
-    pe.matmul(T.ps_lo[0:n, 0:H], T.selown[:, 0:n], T.gat[:, 0:H], start=True, stop=False)
-    pe.matmul(T.ps_hi[0:n, 0:H], T.selown[:, 0:n], T.gat[:, H:M], start=True, stop=False)
+    pe.wait_ge(sem.s_gv1, 1)
+    pe.wait_ge(sem.s_gs1, 1)
+    pe.matmul(T.ps_o[0:n, 0:H], T.selown[:, 0:n], T.gat[:, H:M], start=True, stop=False)
     pe.wait_ge(sem.s_sel, 1)
     pe.wait_ge(sem.s_slots, 16)
-    pe.matmul(T.ps_lo[0:n, 0:H], T.selsum[0:kn, 0:n], T.slots[0:kn, 0:H], start=False, stop=True).then_inc(sem.s_mlo, 1)
-    pe.matmul(T.ps_hi[0:n, 0:H], T.selsum[0:kn, 0:n], T.slots[0:kn, H:M], start=False, stop=True).then_inc(sem.s_mhi, 1)
+    pe.matmul(T.ps_o[0:n, 0:H], T.selsum[0:kn, 0:n], T.slots[0:kn, :], start=False, stop=True).then_inc(sem.s_m, 1)
 
     g.wait_ge(sem.s_one, 1)
     g.affine_select(out=T.rep[0:GRP, :], in_=T.ones[0:GRP, :], pattern=[[0, P // GRP], [-1, GRP]],
@@ -178,6 +225,11 @@ def rank_program(g, core, T, topo):
     g.affine_select(out=T.selown[:, 0:n], in_=T.ones[:, 0:n], pattern=[[-1, n]],
                     compare_op=AluOpType.is_equal, fill=0.0, base=-r0, channel_multiplier=1).then_inc(sem.s_selown, 1)
 
+    g.wait_ge(sem.s_dh, 16)
+    g.remote_dma_fused([RemoteDMATransfer(dst_ids=[_dst(topo, helpers[d])], dma_engine_mask=_to_mask([eng[d]]),
+                                          remote_sem=sem.rsh, src=T.stage_h[d], dst=T.land_h[k])
+                        for d in range(NH)], local_sem=sem.sent)
+
     def scatter(plan):
         trs = []
         for d, e in plan:
@@ -186,8 +238,8 @@ def rank_program(g, core, T, topo):
                 src, dst = T.stage_a[d], T.land_a[slot]
             else:
                 src, dst = T.stage_b[d - NA], T.land_b[slot]
-            trs.append(RemoteDMATransfer(dst_ids=[dst_id(d)], dma_engine_mask=_to_mask(e), remote_sem=sem.rs,
-                                         src=src, dst=dst))
+            trs.append(RemoteDMATransfer(dst_ids=[_dst(topo, cores[d])], dma_engine_mask=_to_mask(e),
+                                         remote_sem=sem.rs, src=src, dst=dst))
         g.remote_dma_fused(trs, local_sem=sem.sent)
 
     g.wait_ge(sem.s_db, 16)
@@ -197,10 +249,10 @@ def rank_program(g, core, T, topo):
 
     g.wait_ge(sem.rs, rs_total)
     others = [d for d in range(N) if d != k]
-    g.remote_dma_fused([RemoteDMATransfer(dst_ids=[dst_id(d) for d in others], dma_engine_mask=_to_mask(eng),
-                                          remote_sem=sem.ag,
+    g.remote_dma_fused([RemoteDMATransfer(dst_ids=[_dst(topo, cores[d]) for d in others],
+                                          dma_engine_mask=_to_mask(eng), remote_sem=sem.ag,
                                           srcs=[my_land[i] for i in range(N - 1)] + [my_stage],
                                           dsts=[my_res for d in others], alu_op=1)],
                        local_sem=sem.sent)
     g.wait_ge(sem.sent, sent_total)
-    g.wait_ge(sem.s_st, 16 * stores)
+    g.wait_ge(sem.s_st, 16 * stores[0])

@@ -7,30 +7,41 @@ P = 128
 TC = 4096
 M = 512
 GRP = 16
+K = M // GRP
+HD = 32
+RB = P - HD
 H = M // 2
 Q = H // 2
 NH = 8
-WH = (P // NH) * H // P
-LOW = P // N
-HIGH = LOW + 1
-NA = P - LOW * N
+WX = HD * M // NH // P
+WH = (RB // NH) * H // P
+NA = 8
 NB = N - NA
+HIGH = 10
+LOW = (RB - NA * HIGH) // NB
 WA = HIGH * H // P
 WB = LOW * H // P
+SPLIT = HD + NA * HIGH
 
 SCRATCH = {
+    "xa": ("sbuf", [P, TC], "float32"),
     "xs": ("sbuf", [P, TC], "float32"),
-    "idxi": ("sbuf", [P, M // GRP], "int32"),
-    "idxf": ("sbuf", [P, M // GRP], "float32"),
-    "off": ("sbuf", [P, M // GRP], "uint16"),
+    "idxi": ("sbuf", [P, K], "int32"),
+    "idxf": ("sbuf", [P, K], "float32"),
+    "offa": ("sbuf", [P, K], "uint16"),
+    "offs": ("sbuf", [P, K], "uint16"),
     "ones": ("sbuf", [P, P], "float32"),
     "rep": ("sbuf", [P, P], "float32"),
     "repn": ("sbuf", [P, (N - 1) * HIGH], "float32"),
     "selown": ("sbuf", [P, HIGH], "float32"),
     "selsum": ("sbuf", [P, HIGH], "float32"),
+    "gata": ("sbuf", [P, M], "float32"),
     "gat": ("sbuf", [P, M], "float32"),
     "slots": ("sbuf", [P, H], "float32"),
     "mine": ("sbuf", [P, H], "float32"),
+    "stage_x": ("dram", [NH, P, WX], "float32"),
+    "land_x": ("dram", [N, P, WX], "float32"),
+    "res_x": ("dram", [NH, P, WX], "float32"),
     "stage_h": ("dram", [NH, P, WH], "float32"),
     "land_h": ("dram", [N, P, WH], "float32"),
     "res_h": ("dram", [NH, P, WH], "float32"),
@@ -44,9 +55,9 @@ SCRATCH = {
     "ps_s": ("psum", [P, M], "float32"),
     "ps_o": ("psum", [P, M], "float32"),
 }
-SEMAPHORES = ["s_idx", "s_x", "s_one", "s_rep", "s_repn", "s_selown", "s_idxf", "s_psi", "s_off", "s_pss", "s_sel",
-              "s_gv0", "s_gs0", "s_gv1", "s_gs1", "s_dh", "s_da", "s_db", "rsh", "agh", "rs", "ag", "sent",
-              "s_slots", "s_m", "s_mine", "s_st"]
+SEMAPHORES = ["s_idx", "s_xa", "s_x", "s_one", "s_rep", "s_repn", "s_selown", "s_idxf", "s_psi", "s_off", "s_pss",
+              "s_sel", "s_gva", "s_gsa", "s_gv0", "s_gs0", "s_gv1", "s_gs1", "s_dx", "s_dh", "s_da", "s_db",
+              "rsx", "agx", "rsh", "agh", "rs", "ag", "sent", "s_slots", "s_m", "s_mine", "s_st"]
 
 
 def _bits(mask):
@@ -60,14 +71,21 @@ def _to_mask(engines):
     return m
 
 
+def _idle(topo, cores, r, taken):
+    c = [h for h in range(NSIM)
+         if h not in cores and h not in taken and topo.chip(h) == topo.chip(cores[r])
+         and topo.die(h) != topo.die(cores[r]) and all(topo.may_write(h, q) for q in cores)]
+    return c[0]
+
+
 def _helpers(topo, cores):
-    out = []
+    half0 = []
     for d in range(NH):
-        c = [h for h in range(NSIM)
-             if h not in cores and topo.chip(h) == topo.chip(cores[d]) and topo.die(h) != topo.die(cores[d])
-             and all(topo.may_write(h, r) for r in cores)]
-        out.append(c[0])
-    return out
+        half0.append(_idle(topo, cores, d, half0))
+    heads = []
+    for d in range(NH):
+        heads.append(_idle(topo, cores, d + N - NH, half0 + heads))
+    return half0, heads
 
 
 def _common(topo, src, dsts):
@@ -81,7 +99,8 @@ def _common(topo, src, dsts):
 
 
 def _engines(topo, cores, r):
-    return _common(topo, cores[r], [c for c in cores if c != cores[r]] + _helpers(topo, cores))
+    half0, heads = _helpers(topo, cores)
+    return _common(topo, cores[r], [c for c in cores if c != cores[r]] + half0 + heads)
 
 
 def _rs_plan(topo, cores, r):
@@ -103,33 +122,35 @@ def _dst(topo, c):
     return DstId(rid=rid, pnc=pid)
 
 
-def helper_program(g, core, T, topo, d):
+def helper_program(g, core, T, topo, d, arrived, land, res, done):
     sem = T.sem
     cores = T.cores
     e = _common(topo, core, cores)
-    g.wait_ge(sem.rsh, N)
+    g.wait_ge(arrived, N)
     g.remote_dma_fused([RemoteDMATransfer(dst_ids=[_dst(topo, c) for c in cores], dma_engine_mask=_to_mask(e),
-                                          remote_sem=sem.agh,
-                                          srcs=[T.land_h[i] for i in range(N)],
-                                          dsts=[T.res_h[d] for c in cores], alu_op=1)],
+                                          remote_sem=done,
+                                          srcs=[land[i] for i in range(N)],
+                                          dsts=[res[d] for c in cores], alu_op=1)],
                        local_sem=sem.sent)
     g.wait_ge(sem.sent, len(e))
 
 
 def rank_program(g, core, T, topo):
     cores = T.cores
-    helpers = _helpers(topo, cores)
+    helpers, heads = _helpers(topo, cores)
     k = T.rank_of(core)
+    sem = T.sem
     if k is None:
         if core in helpers:
-            helper_program(g, core, T, topo, helpers.index(core))
+            helper_program(g, core, T, topo, helpers.index(core), sem.rsh, T.land_h, T.res_h, sem.agh)
+        elif core in heads:
+            helper_program(g, core, T, topo, heads.index(core), sem.rsx, T.land_x, T.res_x, sem.agx)
         return
-    sem = T.sem
     v, s, pe, sy = g.vector, g.scalar, g.tensor, g.sync
 
     wide_owner = k < NA
     n = HIGH if wide_owner else LOW
-    r0 = k * HIGH if wide_owner else NA * HIGH + (k - NA) * LOW
+    r0 = HD + k * HIGH if wide_owner else SPLIT + (k - NA) * LOW
     kn = (N - 1) * n
     my_stage = T.stage_a[k] if wide_owner else T.stage_b[k - NA]
     my_land = T.land_a if wide_owner else T.land_b
@@ -143,70 +164,92 @@ def rank_program(g, core, T, topo):
     wide, narrow = _rs_plan(topo, cores, k)
     eng = _engines(topo, cores, k)
     if len(eng) < NH:
-        raise ValueError("fewer engines than pieces of half 0")
+        raise ValueError("fewer engines than pieces for the helpers")
     ag_total = (N - 1) * len(eng)
     agh_total = sum(len(_common(topo, h, cores)) for h in helpers)
-    sent_total = NH + sum(len(e) for d, e in wide + narrow) + len(eng)
+    agx_total = sum(len(_common(topo, h, cores)) for h in heads)
+    sent_total = 2 * NH + sum(len(e) for d, e in wide + narrow) + len(eng)
     stores = [0]
+    mid = HD + RB // 2
 
-    sy.dma_start(T.xs[0:P // 2, :], T.x[0:P // 2, :]).then_inc(sem.s_x, 16)
+    sy.dma_start(T.xa[0:HD, :], T.x[0:HD, :]).then_inc(sem.s_xa, 16)
+    sy.dma_start(T.xs[mid:P, :], T.x[mid:P, :]).then_inc(sem.s_x, 16)
+    sy.wait_ge(sem.s_gva, 1)
+    sy.wait_ge(sem.s_gsa, 1)
+    sy.dma_start(T.stage_x[:, :, :], T.gata[0:HD, :]).then_inc(sem.s_dx, 16)
     sy.wait_ge(sem.s_gv0, 1)
     sy.wait_ge(sem.s_gs0, 1)
-    sy.dma_start(T.stage_h[:, :, :], T.gat[:, 0:H]).then_inc(sem.s_dh, 16)
+    sy.dma_start(T.stage_h[:, :, :], T.gat[HD:P, 0:H]).then_inc(sem.s_dh, 16)
     sy.wait_ge(sem.s_gv1, 1)
     sy.wait_ge(sem.s_gs1, 1)
-    sy.dma_start(T.stage_a[:, :, :], T.gat[0:NA * HIGH, H:M]).then_inc(sem.s_da, 16)
+    sy.dma_start(T.stage_a[:, :, :], T.gat[HD:SPLIT, H:M]).then_inc(sem.s_da, 16)
     sy.wait_ge(sem.rs, rs_total)
     sy.dma_start(T.slots[0:kn, :], my_land[:, :, :]).then_inc(sem.s_slots, 16)
     sy.wait_ge(sem.agh, agh_total)
-    sy.dma_start(T.y[:, 0:H], T.res_h[:, :, :]).then_inc(sem.s_st, 16)
+    sy.dma_start(T.y[HD:P, 0:H], T.res_h[:, :, :]).then_inc(sem.s_st, 16)
     stores[0] += 1
     sy.wait_ge(sem.s_mine, 1)
     sy.dma_start(T.y[r0:r0 + n, H:M], T.mine[0:n, :]).then_inc(sem.s_st, 16)
     stores[0] += 1
 
     v.memset(T.ones[:, :], 1.0).then_inc(sem.s_one, 1)
+    v.memset(T.offa[HD:2 * HD, :], 0).then_inc(sem.s_off, 1)
+    v.memset(T.offa[2 * HD:P, :], 0).then_inc(sem.s_off, 1)
+    v.memset(T.offs[0:HD, :], 0).then_inc(sem.s_off, 1)
+    v.memset(T.xa[HD:2 * HD, 0:4], 0.0).then_inc(sem.s_off, 1)
+    v.memset(T.xa[2 * HD:P, 0:4], 0.0).then_inc(sem.s_off, 1)
+    v.memset(T.xs[0:HD, 0:4], 0.0).then_inc(sem.s_off, 1)
     v.wait_ge(sem.s_idx, 16)
     v.tensor_copy(T.idxf[0:GRP, :], T.idxi[0:GRP, :]).then_inc(sem.s_idxf, 1)
     v.wait_ge(sem.s_psi, 1)
-    v.tensor_copy(T.off[:, :], T.ps_i[:, 0:M // GRP]).then_inc(sem.s_off, 1)
+    v.tensor_copy(T.offa[0:HD, :], T.ps_i[0:HD, 0:K]).then_inc(sem.s_off, 1)
+    v.tensor_copy(T.offs[HD:2 * HD, :], T.ps_i[HD:2 * HD, 0:K]).then_inc(sem.s_off, 1)
+    v.tensor_copy(T.offs[2 * HD:P, :], T.ps_i[2 * HD:P, 0:K]).then_inc(sem.s_off, 1)
     v.wait_ge(sem.s_pss, 1)
     v.tensor_copy(T.selsum[0:kn, 0:n], T.ps_s[0:kn, 0:n]).then_inc(sem.s_sel, 1)
-    v.wait_ge(sem.s_off, 1)
+    v.wait_ge(sem.s_off, 9)
+    v.wait_ge(sem.s_xa, 16)
+    v.tensor_copy(T.gata[:, 0:H], T.xa[:, 0:TC].indirect(T.offa[:, 0:K // 2])).then_inc(sem.s_gva, 1)
     v.wait_ge(sem.s_x, 32)
     for c, done in ((0, sem.s_gv0), (1, sem.s_gv1)):
         j = c * H
         v.tensor_copy(T.gat[:, j:j + Q],
-                      T.xs[:, 0:TC].indirect(T.off[:, j // GRP:(j + Q) // GRP])).then_inc(done, 1)
+                      T.xs[:, 0:TC].indirect(T.offs[:, j // GRP:(j + Q) // GRP])).then_inc(done, 1)
     v.wait_ge(sem.s_m, 1)
     v.tensor_copy(T.mine[0:n, :], T.ps_o[0:n, 0:H]).then_inc(sem.s_mine, 1)
 
     s.dma_start(T.idxi[0:GRP, :], T.idx[:, :]).then_inc(sem.s_idx, 16)
-    s.dma_start(T.xs[P // 2:P, :], T.x[P // 2:P, :]).then_inc(sem.s_x, 16)
-    s.wait_ge(sem.s_off, 1)
+    s.dma_start(T.xs[HD:mid, :], T.x[HD:mid, :]).then_inc(sem.s_x, 16)
+    s.wait_ge(sem.s_off, 9)
+    s.wait_ge(sem.s_xa, 16)
+    s.activation(T.gata[:, H:M], T.xa[:, 0:TC].indirect(T.offa[:, K // 2:K]),
+                 ActivationFunctionType.Copy).then_inc(sem.s_gsa, 1)
     s.wait_ge(sem.s_x, 32)
     for c, done in ((0, sem.s_gs0), (1, sem.s_gs1)):
         j = c * H + Q
-        s.activation(T.gat[:, j:j + Q], T.xs[:, 0:TC].indirect(T.off[:, j // GRP:(j + Q) // GRP]),
+        s.activation(T.gat[:, j:j + Q], T.xs[:, 0:TC].indirect(T.offs[:, j // GRP:(j + Q) // GRP]),
                      ActivationFunctionType.Copy).then_inc(done, 1)
     s.wait_ge(sem.s_gs1, 1)
     s.wait_ge(sem.s_gv1, 1)
-    s.dma_start(T.stage_b[:, :, :], T.gat[NA * HIGH:P, H:M]).then_inc(sem.s_db, 16)
+    s.dma_start(T.stage_b[:, :, :], T.gat[SPLIT:P, H:M]).then_inc(sem.s_db, 16)
+    s.wait_ge(sem.agx, agx_total)
+    s.dma_start(T.y[0:HD, :], T.res_x[:, :, :]).then_inc(sem.s_st, 16)
+    stores[0] += 1
     s.wait_ge(sem.ag, ag_total)
     runs_a = [(0, k), (k + 1, NA)] if wide_owner else [(0, NA)]
     runs_a = sorted([x for x in runs_a if x[1] > x[0]], key=lambda x: x[0] - x[1])
     for lo, hi in runs_a:
-        s.dma_start(T.y[lo * HIGH:hi * HIGH, H:M], T.res_a[lo:hi]).then_inc(sem.s_st, 16)
+        s.dma_start(T.y[HD + lo * HIGH:HD + hi * HIGH, H:M], T.res_a[lo:hi]).then_inc(sem.s_st, 16)
         stores[0] += 1
     runs_b = [(0, NB)] if wide_owner else [(0, k - NA), (k - NA + 1, NB)]
     for lo, hi in runs_b:
         if hi > lo:
-            s.dma_start(T.y[NA * HIGH + lo * LOW:NA * HIGH + hi * LOW, H:M], T.res_b[lo:hi]).then_inc(sem.s_st, 16)
+            s.dma_start(T.y[SPLIT + lo * LOW:SPLIT + hi * LOW, H:M], T.res_b[lo:hi]).then_inc(sem.s_st, 16)
             stores[0] += 1
 
     pe.wait_ge(sem.s_rep, 1)
     pe.wait_ge(sem.s_idxf, 1)
-    pe.matmul(T.ps_i[:, 0:M // GRP], T.rep[0:GRP, :], T.idxf[0:GRP, :], start=True, stop=True).then_inc(sem.s_psi, 1)
+    pe.matmul(T.ps_i[:, 0:K], T.rep[0:GRP, :], T.idxf[0:GRP, :], start=True, stop=True).then_inc(sem.s_psi, 1)
     pe.wait_ge(sem.s_repn, 1)
     pe.matmul(T.ps_s[0:kn, 0:n], T.repn[0:n, 0:kn], T.repn[0:n, 0:n], start=True, stop=True).then_inc(sem.s_pss, 1)
     pe.wait_ge(sem.s_selown, 1)
@@ -225,10 +268,12 @@ def rank_program(g, core, T, topo):
     g.affine_select(out=T.selown[:, 0:n], in_=T.ones[:, 0:n], pattern=[[-1, n]],
                     compare_op=AluOpType.is_equal, fill=0.0, base=-r0, channel_multiplier=1).then_inc(sem.s_selown, 1)
 
-    g.wait_ge(sem.s_dh, 16)
-    g.remote_dma_fused([RemoteDMATransfer(dst_ids=[_dst(topo, helpers[d])], dma_engine_mask=_to_mask([eng[d]]),
-                                          remote_sem=sem.rsh, src=T.stage_h[d], dst=T.land_h[k])
-                        for d in range(NH)], local_sem=sem.sent)
+    for staged, stage, land, arrived, hs in ((sem.s_dx, T.stage_x, T.land_x, sem.rsx, heads),
+                                             (sem.s_dh, T.stage_h, T.land_h, sem.rsh, helpers)):
+        g.wait_ge(staged, 16)
+        g.remote_dma_fused([RemoteDMATransfer(dst_ids=[_dst(topo, hs[d])], dma_engine_mask=_to_mask([eng[d]]),
+                                              remote_sem=arrived, src=stage[d], dst=land[k])
+                            for d in range(NH)], local_sem=sem.sent)
 
     def scatter(plan):
         trs = []

from concourse.bass import DstId, RemoteDMATransfer
from concourse.mybir import AluOpType, ActivationFunctionType

N = 10
NSIM = 112
P = 128
TC = 4096
M = 512
GRP = 16
K = M // GRP
HD = 32
RB = P - HD
H = M // 2
Q = H // 2
NH = 8
WX = HD * M // NH // P
WH = (RB // NH) * H // P
NA = 8
NB = N - NA
HIGH = 10
LOW = (RB - NA * HIGH) // NB
WA = HIGH * H // P
WB = LOW * H // P
SPLIT = HD + NA * HIGH

SCRATCH = {
    "xa": ("sbuf", [P, TC], "float32"),
    "xs": ("sbuf", [P, TC], "float32"),
    "idxi": ("sbuf", [P, K], "int32"),
    "idxf": ("sbuf", [P, K], "float32"),
    "offa": ("sbuf", [P, K], "uint16"),
    "offs": ("sbuf", [P, K], "uint16"),
    "ones": ("sbuf", [P, P], "float32"),
    "rep": ("sbuf", [P, P], "float32"),
    "repn": ("sbuf", [P, (N - 1) * HIGH], "float32"),
    "selown": ("sbuf", [P, HIGH], "float32"),
    "selsum": ("sbuf", [P, HIGH], "float32"),
    "gata": ("sbuf", [P, M], "float32"),
    "gat": ("sbuf", [P, M], "float32"),
    "slots": ("sbuf", [P, H], "float32"),
    "mine": ("sbuf", [P, H], "float32"),
    "stage_x": ("dram", [NH, P, WX], "float32"),
    "land_x": ("dram", [N, P, WX], "float32"),
    "res_x": ("dram", [NH, P, WX], "float32"),
    "stage_h": ("dram", [NH, P, WH], "float32"),
    "land_h": ("dram", [N, P, WH], "float32"),
    "res_h": ("dram", [NH, P, WH], "float32"),
    "stage_a": ("dram", [NA, P, WA], "float32"),
    "stage_b": ("dram", [NB, P, WB], "float32"),
    "land_a": ("dram", [N - 1, P, WA], "float32"),
    "land_b": ("dram", [N - 1, P, WB], "float32"),
    "res_a": ("dram", [NA, P, WA], "float32"),
    "res_b": ("dram", [NB, P, WB], "float32"),
    "ps_i": ("psum", [P, M], "float32"),
    "ps_s": ("psum", [P, M], "float32"),
    "ps_o": ("psum", [P, M], "float32"),
}
SEMAPHORES = ["s_idx", "s_xa", "s_x", "s_one", "s_rep", "s_repn", "s_selown", "s_idxf", "s_psi", "s_off", "s_pss",
              "s_sel", "s_gva", "s_gsa", "s_gv0", "s_gs0", "s_gv1", "s_gs1", "s_dx", "s_dh", "s_da", "s_db",
              "rsx", "agx", "rsh", "agh", "rs", "ag", "sent", "s_slots", "s_m", "s_mine", "s_st"]


def _bits(mask):
    return [b for b in range(16) if (mask >> b) & 1]


def _to_mask(engines):
    m = 0
    for b in engines:
        m |= 1 << b
    return m


def _idle(topo, cores, r, taken):
    c = [h for h in range(NSIM)
         if h not in cores and h not in taken and topo.chip(h) == topo.chip(cores[r])
         and topo.die(h) != topo.die(cores[r]) and all(topo.may_write(h, q) for q in cores)]
    return c[0]


def _helpers(topo, cores):
    half0 = []
    for d in range(NH):
        half0.append(_idle(topo, cores, d, half0))
    heads = []
    for d in range(NH):
        heads.append(_idle(topo, cores, d + N - NH, half0 + heads))
    return half0, heads


def _common(topo, src, dsts):
    m = None
    for d in dsts:
        if not topo.may_write(src, d):
            raise ValueError("core %d may not write to core %d" % (src, d))
        mm = topo.mask(src, d)
        m = mm if m is None else (m & mm)
    return _bits(m)


def _engines(topo, cores, r):
    half0, heads = _helpers(topo, cores)
    return _common(topo, cores[r], [c for c in cores if c != cores[r]] + half0 + heads)


def _rs_plan(topo, cores, r):
    e = _engines(topo, cores, r)
    a = [d for d in range(NA) if d != r]
    b = [d for d in range(NA, N) if d != r]
    wide = [(d, [e[i]]) for i, d in enumerate(a)]
    if len(b) == 1:
        narrow = [(b[0], list(e))]
    else:
        o = b if r % 2 == 0 else b[::-1]
        narrow = [(o[0], e[len(a):len(a) + 1]),
                  (o[1], e[0::2])]
    return wide, narrow


def _dst(topo, c):
    rid, pid, _ = topo.addr(c)
    return DstId(rid=rid, pnc=pid)


def helper_program(g, core, T, topo, d, arrived, land, res, done):
    sem = T.sem
    cores = T.cores
    e = _common(topo, core, cores)
    g.wait_ge(arrived, N)
    g.remote_dma_fused([RemoteDMATransfer(dst_ids=[_dst(topo, c) for c in cores], dma_engine_mask=_to_mask(e),
                                          remote_sem=done,
                                          srcs=[land[i] for i in range(N)],
                                          dsts=[res[d] for c in cores], alu_op=1)],
                       local_sem=sem.sent)
    g.wait_ge(sem.sent, len(e))


def rank_program(g, core, T, topo):
    cores = T.cores
    helpers, heads = _helpers(topo, cores)
    k = T.rank_of(core)
    sem = T.sem
    if k is None:
        if core in helpers:
            helper_program(g, core, T, topo, helpers.index(core), sem.rsh, T.land_h, T.res_h, sem.agh)
        elif core in heads:
            helper_program(g, core, T, topo, heads.index(core), sem.rsx, T.land_x, T.res_x, sem.agx)
        return
    v, s, pe, sy = g.vector, g.scalar, g.tensor, g.sync

    wide_owner = k < NA
    n = HIGH if wide_owner else LOW
    r0 = HD + k * HIGH if wide_owner else SPLIT + (k - NA) * LOW
    kn = (N - 1) * n
    my_stage = T.stage_a[k] if wide_owner else T.stage_b[k - NA]
    my_land = T.land_a if wide_owner else T.land_b
    my_res = T.res_a[k] if wide_owner else T.res_b[k - NA]

    rs_total = 0
    for r in range(N):
        if r != k:
            w_, n_ = _rs_plan(topo, cores, r)
            rs_total += sum(len(e) for d, e in w_ + n_ if d == k)
    wide, narrow = _rs_plan(topo, cores, k)
    eng = _engines(topo, cores, k)
    if len(eng) < NH:
        raise ValueError("fewer engines than pieces for the helpers")
    ag_total = (N - 1) * len(eng)
    agh_total = sum(len(_common(topo, h, cores)) for h in helpers)
    agx_total = sum(len(_common(topo, h, cores)) for h in heads)
    sent_total = 2 * NH + sum(len(e) for d, e in wide + narrow) + len(eng)
    stores = [0]
    mid = HD + RB // 2

    sy.dma_start(T.xa[0:HD, :], T.x[0:HD, :]).then_inc(sem.s_xa, 16)
    sy.dma_start(T.xs[mid:P, :], T.x[mid:P, :]).then_inc(sem.s_x, 16)
    sy.wait_ge(sem.s_gva, 1)
    sy.wait_ge(sem.s_gsa, 1)
    sy.dma_start(T.stage_x[:, :, :], T.gata[0:HD, :]).then_inc(sem.s_dx, 16)
    sy.wait_ge(sem.s_gv0, 1)
    sy.wait_ge(sem.s_gs0, 1)
    sy.dma_start(T.stage_h[:, :, :], T.gat[HD:P, 0:H]).then_inc(sem.s_dh, 16)
    sy.wait_ge(sem.s_gv1, 1)
    sy.wait_ge(sem.s_gs1, 1)
    sy.dma_start(T.stage_a[:, :, :], T.gat[HD:SPLIT, H:M]).then_inc(sem.s_da, 16)
    sy.wait_ge(sem.rs, rs_total)
    sy.dma_start(T.slots[0:kn, :], my_land[:, :, :]).then_inc(sem.s_slots, 16)
    sy.wait_ge(sem.agh, agh_total)
    sy.dma_start(T.y[HD:P, 0:H], T.res_h[:, :, :]).then_inc(sem.s_st, 16)
    stores[0] += 1
    sy.wait_ge(sem.s_mine, 1)
    sy.dma_start(T.y[r0:r0 + n, H:M], T.mine[0:n, :]).then_inc(sem.s_st, 16)
    stores[0] += 1

    v.memset(T.ones[:, :], 1.0).then_inc(sem.s_one, 1)
    v.memset(T.offa[HD:2 * HD, :], 0).then_inc(sem.s_off, 1)
    v.memset(T.offa[2 * HD:P, :], 0).then_inc(sem.s_off, 1)
    v.memset(T.offs[0:HD, :], 0).then_inc(sem.s_off, 1)
    v.memset(T.xa[HD:2 * HD, 0:4], 0.0).then_inc(sem.s_off, 1)
    v.memset(T.xa[2 * HD:P, 0:4], 0.0).then_inc(sem.s_off, 1)
    v.memset(T.xs[0:HD, 0:4], 0.0).then_inc(sem.s_off, 1)
    v.wait_ge(sem.s_idx, 16)
    v.tensor_copy(T.idxf[0:GRP, :], T.idxi[0:GRP, :]).then_inc(sem.s_idxf, 1)
    v.wait_ge(sem.s_psi, 1)
    v.tensor_copy(T.offa[0:HD, :], T.ps_i[0:HD, 0:K]).then_inc(sem.s_off, 1)
    v.tensor_copy(T.offs[HD:2 * HD, :], T.ps_i[HD:2 * HD, 0:K]).then_inc(sem.s_off, 1)
    v.tensor_copy(T.offs[2 * HD:P, :], T.ps_i[2 * HD:P, 0:K]).then_inc(sem.s_off, 1)
    v.wait_ge(sem.s_pss, 1)
    v.tensor_copy(T.selsum[0:kn, 0:n], T.ps_s[0:kn, 0:n]).then_inc(sem.s_sel, 1)
    v.wait_ge(sem.s_off, 9)
    v.wait_ge(sem.s_xa, 16)
    v.tensor_copy(T.gata[:, 0:H], T.xa[:, 0:TC].indirect(T.offa[:, 0:K // 2])).then_inc(sem.s_gva, 1)
    v.wait_ge(sem.s_x, 32)
    for c, done in ((0, sem.s_gv0), (1, sem.s_gv1)):
        j = c * H
        v.tensor_copy(T.gat[:, j:j + Q],
                      T.xs[:, 0:TC].indirect(T.offs[:, j // GRP:(j + Q) // GRP])).then_inc(done, 1)
    v.wait_ge(sem.s_m, 1)
    v.tensor_copy(T.mine[0:n, :], T.ps_o[0:n, 0:H]).then_inc(sem.s_mine, 1)

    s.dma_start(T.idxi[0:GRP, :], T.idx[:, :]).then_inc(sem.s_idx, 16)
    s.dma_start(T.xs[HD:mid, :], T.x[HD:mid, :]).then_inc(sem.s_x, 16)
    s.wait_ge(sem.s_off, 9)
    s.wait_ge(sem.s_xa, 16)
    s.activation(T.gata[:, H:M], T.xa[:, 0:TC].indirect(T.offa[:, K // 2:K]),
                 ActivationFunctionType.Copy).then_inc(sem.s_gsa, 1)
    s.wait_ge(sem.s_x, 32)
    for c, done in ((0, sem.s_gs0), (1, sem.s_gs1)):
        j = c * H + Q
        s.activation(T.gat[:, j:j + Q], T.xs[:, 0:TC].indirect(T.offs[:, j // GRP:(j + Q) // GRP]),
                     ActivationFunctionType.Copy).then_inc(done, 1)
    s.wait_ge(sem.s_gs1, 1)
    s.wait_ge(sem.s_gv1, 1)
    s.dma_start(T.stage_b[:, :, :], T.gat[SPLIT:P, H:M]).then_inc(sem.s_db, 16)
    s.wait_ge(sem.agx, agx_total)
    s.dma_start(T.y[0:HD, :], T.res_x[:, :, :]).then_inc(sem.s_st, 16)
    stores[0] += 1
    s.wait_ge(sem.ag, ag_total)
    runs_a = [(0, k), (k + 1, NA)] if wide_owner else [(0, NA)]
    runs_a = sorted([x for x in runs_a if x[1] > x[0]], key=lambda x: x[0] - x[1])
    for lo, hi in runs_a:
        s.dma_start(T.y[HD + lo * HIGH:HD + hi * HIGH, H:M], T.res_a[lo:hi]).then_inc(sem.s_st, 16)
        stores[0] += 1
    runs_b = [(0, NB)] if wide_owner else [(0, k - NA), (k - NA + 1, NB)]
    for lo, hi in runs_b:
        if hi > lo:
            s.dma_start(T.y[SPLIT + lo * LOW:SPLIT + hi * LOW, H:M], T.res_b[lo:hi]).then_inc(sem.s_st, 16)
            stores[0] += 1

    pe.wait_ge(sem.s_rep, 1)
    pe.wait_ge(sem.s_idxf, 1)
    pe.matmul(T.ps_i[:, 0:K], T.rep[0:GRP, :], T.idxf[0:GRP, :], start=True, stop=True).then_inc(sem.s_psi, 1)
    pe.wait_ge(sem.s_repn, 1)
    pe.matmul(T.ps_s[0:kn, 0:n], T.repn[0:n, 0:kn], T.repn[0:n, 0:n], start=True, stop=True).then_inc(sem.s_pss, 1)
    pe.wait_ge(sem.s_selown, 1)
    pe.wait_ge(sem.s_gv1, 1)
    pe.wait_ge(sem.s_gs1, 1)
    pe.matmul(T.ps_o[0:n, 0:H], T.selown[:, 0:n], T.gat[:, H:M], start=True, stop=False)
    pe.wait_ge(sem.s_sel, 1)
    pe.wait_ge(sem.s_slots, 16)
    pe.matmul(T.ps_o[0:n, 0:H], T.selsum[0:kn, 0:n], T.slots[0:kn, :], start=False, stop=True).then_inc(sem.s_m, 1)

    g.wait_ge(sem.s_one, 1)
    g.affine_select(out=T.rep[0:GRP, :], in_=T.ones[0:GRP, :], pattern=[[0, P // GRP], [-1, GRP]],
                    compare_op=AluOpType.is_equal, fill=0.0, base=0, channel_multiplier=1).then_inc(sem.s_rep, 1)
    g.affine_select(out=T.repn[0:n, 0:kn], in_=T.ones[0:n, 0:kn], pattern=[[0, N - 1], [-1, n]],
                    compare_op=AluOpType.is_equal, fill=0.0, base=0, channel_multiplier=1).then_inc(sem.s_repn, 1)
    g.affine_select(out=T.selown[:, 0:n], in_=T.ones[:, 0:n], pattern=[[-1, n]],
                    compare_op=AluOpType.is_equal, fill=0.0, base=-r0, channel_multiplier=1).then_inc(sem.s_selown, 1)

    for staged, stage, land, arrived, hs in ((sem.s_dx, T.stage_x, T.land_x, sem.rsx, heads),
                                             (sem.s_dh, T.stage_h, T.land_h, sem.rsh, helpers)):
        g.wait_ge(staged, 16)
        g.remote_dma_fused([RemoteDMATransfer(dst_ids=[_dst(topo, hs[d])], dma_engine_mask=_to_mask([eng[d]]),
                                              remote_sem=arrived, src=stage[d], dst=land[k])
                            for d in range(NH)], local_sem=sem.sent)

    def scatter(plan):
        trs = []
        for d, e in plan:
            slot = k if k < d else k - 1
            if d < NA:
                src, dst = T.stage_a[d], T.land_a[slot]
            else:
                src, dst = T.stage_b[d - NA], T.land_b[slot]
            trs.append(RemoteDMATransfer(dst_ids=[_dst(topo, cores[d])], dma_engine_mask=_to_mask(e),
                                         remote_sem=sem.rs, src=src, dst=dst))
        g.remote_dma_fused(trs, local_sem=sem.sent)

    g.wait_ge(sem.s_db, 16)
    scatter(narrow)
    g.wait_ge(sem.s_da, 16)
    scatter(wide)

    g.wait_ge(sem.rs, rs_total)
    others = [d for d in range(N) if d != k]
    g.remote_dma_fused([RemoteDMATransfer(dst_ids=[_dst(topo, cores[d]) for d in others],
                                          dma_engine_mask=_to_mask(eng), remote_sem=sem.ag,
                                          srcs=[my_land[i] for i in range(N - 1)] + [my_stage],
                                          dsts=[my_res for d in others], alu_op=1)],
                       local_sem=sem.sent)
    g.wait_ge(sem.sent, sent_total)
    g.wait_ge(sem.s_st, 16 * stores[0])
